import numpy as np
import ml_dtypes


def mxq(x, axis, fmt="e4m3"):
    dtype, down = {"e4m3": (ml_dtypes.float8_e4m3fn, 7), "e5m2": (ml_dtypes.float8_e5m2, 14)}[fmt]
    v = np.moveaxis(np.asarray(x, np.float32).astype(ml_dtypes.bfloat16).astype(np.float64), axis, -1)
    blocks = v.reshape(v.shape[:-1] + (-1, 32))
    amax = np.abs(blocks).max(-1, keepdims=True)
    byte = np.maximum(np.where(amax > 0, np.frexp(amax)[1] - 1 + 127, 0) - down, 1)
    scale = np.exp2(byte - 127.0)
    codes = (blocks / scale).astype(np.float32).astype(dtype).astype(np.float64)
    return np.moveaxis((codes * scale).reshape(v.shape), -1, axis)


WIDE = False


def mx_kscale(k):
    if not WIDE:
        return np.ones(k)
    levels = np.array([30, -30])
    if k % 512:
        return np.exp2(np.random.permutation(np.resize(levels, k // 32))).repeat(32)
    a = np.empty((k // 512, 16))
    for p in range(k // 512):
        a[p, :8] = np.random.permutation(np.resize(levels, 8))
        for g in range(8):
            far = levels[np.abs(levels - a[p, g]) >= 10]
            a[p, g + 8] = far[np.random.randint(len(far))]
    return np.exp2(a.ravel()).repeat(32)


def f64(x):
    return np.asarray(x).astype(np.float64)


def striped(idx):
    return np.tile(np.asarray(idx).reshape(-1, 16).T, (8, 1)).astype(np.uint16)


def unstriped(offs):
    return offs[:16].T.reshape(-1).astype(np.int64)


E2M1 = np.array([0.0, 0.5, 1.0, 1.5, 2.0, 3.0, 4.0, 6.0, -0.0, -0.5, -1.0, -1.5, -2.0, -3.0, -4.0, -6.0])


def pack_weight(w, fmt):
    k, n = w.shape
    w = f64(np.asarray(w, np.float32).astype(ml_dtypes.bfloat16)).reshape(k // 32, 32, n)
    amax = np.abs(w).max(1)
    if fmt == "e4m3":
        byte = np.frexp(amax)[1] - 1 + 127 - 7
    else:
        mant, ex = np.frexp(amax / 6.0)
        byte = np.where(mant > 0.5, ex, ex - 1) + 127
    byte = np.clip(np.where(amax > 0, byte, 1), 1, 254)
    scaled = (w * np.exp2(127.0 - byte)[:, None, :]).reshape(k, n).astype(np.float32)
    by_word = np.ascontiguousarray(scaled.reshape(k // 512, 128, 4, n).transpose(0, 1, 3, 2))
    if fmt == "e4m3":
        words = by_word.astype(ml_dtypes.float8_e4m3fn).view(np.uint8)
    else:
        c = by_word.astype(ml_dtypes.float4_e2m1fn).view(np.uint8) & 0xF
        words = (c[..., 0::2] | (c[..., 1::2] << 4)).reshape(k // 512, 128, 2 * n)
    return np.ascontiguousarray(words), np.ascontiguousarray(byte.astype(np.uint8).reshape(k // 512, 16, n))


def unpack_weight(words, scales, fmt):
    g, _, n = scales.shape
    words = np.ascontiguousarray(words).reshape(g, 128, n, -1)
    if fmt == "e4m3":
        vals = words.view(ml_dtypes.float8_e4m3fn).astype(np.float64)
    else:
        nib = np.empty((g, 128, n, 4), np.uint8)
        nib[..., 0::2] = words & 0xF
        nib[..., 1::2] = words >> 4
        vals = E2M1[nib]
    vals = vals * np.repeat(np.exp2(scales.astype(np.float64) - 127.0), 8, axis=1)[..., None]
    return vals.transpose(0, 1, 3, 2).reshape(g * 512, n)


K, T, J, R, O, N, L, E = 512, 2048, 256, 512, 128, 256, 512, 1024


def setup_inputs():
    n = np.random.standard_normal
    idx = np.random.permutation(T)[:J]
    idx2 = np.random.permutation(T)[:J]
    idx3 = np.random.permutation(T)[:J]
    idx4 = np.random.permutation(J)[:O]
    idx5 = np.random.permutation(J)[:O]
    idx6 = np.random.permutation(E)[:O]
    fk = mx_kscale(K)
    fr = mx_kscale(R)
    fl = mx_kscale(L)
    xtp = pack_weight(n((K, T)) / fk[:, None], "e2m1")
    wp = pack_weight(n((K, R)) * 1 / np.sqrt(K) * fk[:, None] * fr, "e4m3")
    wbp = pack_weight(n((R, N)) * 1 / np.sqrt(R) / fr[:, None], "e2m1")
    sxp = pack_weight(n((L, O)) / fl[:, None], "e4m3")
    wsp = pack_weight(n((L, N)) * 1 / np.sqrt(L) * fl[:, None], "e4m3")
    return {
        "xt_words": xtp[0],
        "xt_scales": xtp[1],
        "w_words": wp[0],
        "w_scales": wp[1],
        "wb_words": wbp[0],
        "wb_scales": wbp[1],
        "sx_words": sxp[0],
        "sx_scales": sxp[1],
        "ws_words": wsp[0],
        "ws_scales": wsp[1],
        "tz": (n((N, E))).astype(np.float32),
        "offs": striped(idx),
        "offs2": striped(idx2),
        "offs3": striped(idx3),
        "offs4": striped(idx4),
        "offs5": striped(idx5),
        "offs6": striped(idx6),
    }


def reference(xt_words, xt_scales, w_words, w_scales, wb_words, wb_scales, sx_words, sx_scales, ws_words, ws_scales, tz, offs, offs2, offs3, offs4, offs5, offs6):
    idx = unstriped(offs)
    idx2 = unstriped(offs2)
    idx3 = unstriped(offs3)
    idx4 = unstriped(offs4)
    idx5 = unstriped(offs5)
    idx6 = unstriped(offs6)
    xtu = unpack_weight(xt_words, xt_scales, "e2m1")
    wu = unpack_weight(w_words, w_scales, "e4m3")
    wbu = unpack_weight(wb_words, wb_scales, "e2m1")
    sxu = unpack_weight(sx_words, sx_scales, "e4m3")
    wsu = unpack_weight(ws_words, ws_scales, "e4m3")
    xtidxg = xtu[:, idx]
    a = wu.T @ xtidxg
    xtidx2g = xtu[:, idx2]
    b = wu.T @ xtidx2g
    xtidx3g = xtu[:, idx3]
    g0 = wu.T @ xtidx3g
    c1 = np.maximum(b, g0)
    hid = np.maximum(a[:, idx4], c1[:, idx5])
    hidq = mxq(hid, 0, "e5m2")
    p = wbu.T @ hidq + wsu.T @ sxu
    y = p + f64(tz)[:, idx6]
    return y

@@ -1,0 +1,152 @@
+from contextlib import ExitStack
+
+import concourse.mybir as mybir
+
+K, T, J, R, O, N, L, E = 512, 2048, 256, 512, 128, 256, 512, 1024
+FLOPS = 2 * (3 * K * R * J + R * N * O + L * N * O)
+
+F32 = mybir.dt.float32
+BF16 = mybir.dt.bfloat16
+I32 = mybir.dt.int32
+U32 = mybir.dt.uint32
+U16 = mybir.dt.uint16
+U8 = mybir.dt.uint8
+E4M3 = mybir.dt.float8_e4m3fn_x4
+E5M2 = mybir.dt.float8_e5m2_x4
+E2M1 = mybir.dt.float4_e2m1fn_x4
+COPY = mybir.ActivationFunctionType.Copy
+MAX = mybir.AluOpType.max
+ADD = mybir.AluOpType.add
+P = 128
+PACK = 4
+
+
+def load_scales(queue, plane, rows):
+    by_row = rows[0].bitcast(I32).rearrange("(q i) c -> i q c", i=4)
+    for i in range(4):
+        queue.dma_start(out=plane[:].bitcast(I32)[i:P:32, :], in_=by_row[i])
+
+
+def tile_list_triple_looked_skip_tabled_kernel(
+    tc, xt_words, xt_scales, w_words, w_scales, wb_words, wb_scales, sx_words, sx_scales,
+    ws_words, ws_scales, tz, offs, offs2, offs3, offs4, offs5, offs6, out,
+):
+    nc = tc.nc
+    with ExitStack() as ctx:
+        lists = ctx.enter_context(tc.tile_pool(name="lists", bufs=1))
+        sb = ctx.enter_context(tc.tile_pool(name="sb", bufs=1))
+        ps = ctx.enter_context(tc.psum_pool(name="ps", bufs=1))
+
+        la = lists.tile([P, J // 16], U16, name="la")
+        lb = lists.tile([P, J // 16], U16, name="lb")
+        lg = lists.tile([P, J // 16], U16, name="lg")
+        l4 = lists.tile([P, O // 16], U16, name="l4")
+        l5 = lists.tile([P, O // 16], U16, name="l5")
+        l6 = lists.tile([P, O // 16], U16, name="l6")
+
+        xw = sb.tile([P, T], U16, name="xw", align_bytes=64)
+        xs = sb.tile([P, T], U8, name="xs", align_bytes=64)
+        w_raw = sb.tile([P, R], U32, name="w_raw", align_bytes=64)
+        wsc_raw = sb.tile([P, R], U8, name="wsc_raw", align_bytes=64)
+        wq = sb.tile([P, R], U32, name="wq", align_bytes=64)
+        wsc = sb.tile([P, R], U8, name="wsc", align_bytes=64)
+        wbw = sb.tile([P, N], U16, name="wbw", align_bytes=64)
+        wbs = sb.tile([P, N], U8, name="wbs", align_bytes=64)
+        sxw = sb.tile([P, O], U32, name="sxw", align_bytes=64)
+        sxs = sb.tile([P, O], U8, name="sxs", align_bytes=64)
+        wsw = sb.tile([P, N], U32, name="wsw", align_bytes=64)
+        wss = sb.tile([P, N], U8, name="wss", align_bytes=64)
+        tzt = [sb.tile([P, E], F32, name="tz%d" % h) for h in range(2)]
+
+        for plane in (wsc_raw, xs, wss, sxs, wbs):
+            nc.vector.memset(plane[:].bitcast(I32), 0)
+
+        nc.sync.dma_start(lb[:], offs2)
+        load_scales(nc.sync, wsc_raw, w_scales)
+        nc.scalar.dma_start(out=xw[:].bitcast(I32), in_=xt_words[0].bitcast(I32))
+        nc.scalar.dma_start(out=w_raw[:].bitcast(I32), in_=w_words[0].rearrange("p n t -> p (n t)").bitcast(I32))
+        nc.sync.dma_start(la[:], offs)
+        load_scales(nc.sync, xs, xt_scales)
+        nc.sync.dma_start(lg[:], offs3)
+        nc.sync.dma_start(l4[:], offs4)
+        nc.sync.dma_start(l5[:], offs5)
+        nc.sync.dma_start(l6[:], offs6)
+        load_scales(nc.sync, wss, ws_scales)
+        load_scales(nc.sync, sxs, sx_scales)
+        load_scales(nc.sync, wbs, wb_scales)
+        nc.sync.dma_start(out=wsw[:].bitcast(I32), in_=ws_words[0].rearrange("p n t -> p (n t)").bitcast(I32))
+        nc.sync.dma_start(out=sxw[:].bitcast(I32), in_=sx_words[0].rearrange("p n t -> p (n t)").bitcast(I32))
+        nc.sync.dma_start(out=wbw[:].bitcast(I32), in_=wb_words[0].bitcast(I32))
+        for h in range(2):
+            nc.sync.dma_start(out=tzt[h][:], in_=tz[h * P:(h + 1) * P, :])
+
+        nc.vector.tensor_copy(out=wsc[:].rearrange("p (t m) -> p t m", t=PACK), in_=wsc_raw[:].rearrange("p (m t) -> p t m", t=PACK))
+        nc.scalar.copy(out=wq[:].rearrange("p (t m) -> p m t", t=PACK), in_=w_raw[:].rearrange("p (m t) -> p m t", t=PACK))
+
+        def first_stage(name, lst):
+            gw = sb.tile([P, J], U16, name="gw_" + name, align_bytes=64)
+            gs = sb.tile([P, J], U8, name="gs_" + name, align_bytes=64)
+            nc.vector.tensor_copy(out=gw[:], in_=xw[:].indirect(lst[:]))
+            nc.vector.tensor_copy(out=gs[:], in_=xs[:].indirect(lst[:]))
+            banks = []
+            for u in range(2):
+                bank = ps.tile([P, 2 * J], F32, name="bank_%s%d" % (name, u))
+                for v in range(2):
+                    cols = slice((2 * u + v) * P, (2 * u + v + 1) * P)
+                    nc.tensor.matmul_mx(out=bank[:, v * J:(v + 1) * J], lhsT=wq[:, cols].bitcast(E4M3), lhsT_scale=wsc[:, cols],
+                                        rhs=gw[:].bitcast(E2M1), rhs_scale=gs[:], start=True, stop=True)
+                banks.append(bank)
+            return banks
+
+        b_banks = first_stage("b", lb)
+        b_sb = [sb.tile([P, 2 * J], F32, name="b_sb%d" % u) for u in range(2)]
+        for u in range(2):
+            nc.scalar.copy(out=b_sb[u][:], in_=b_banks[u][:])
+        a_banks = first_stage("a", la)
+        a_sb = [sb.tile([P, 2 * J], F32, name="a_sb%d" % u) for u in range(2)]
+        for u in range(2):
+            nc.scalar.copy(out=a_sb[u][:], in_=a_banks[u][:])
+        g_banks = first_stage("g", lg)
+
+        a_pick = sb.tile([P, PACK, O], F32, name="a_pick")
+        c_pick = sb.tile([P, PACK, O], F32, name="c_pick")
+
+        def pick(on_vector, dst, window, lst):
+            if on_vector:
+                nc.vector.tensor_copy(out=dst, in_=window.indirect(lst[:]))
+            else:
+                nc.scalar.activation(out=dst, in_=window.indirect(lst[:]), func=COPY)
+
+        for t in range(PACK):
+            pick(t < 2, a_pick[:, t, :], a_sb[t // 2][:, (t % 2) * J:(t % 2 + 1) * J], l4)
+        c_sb = [sb.tile([P, 2 * J], F32, name="c_sb%d" % u) for u in range(2)]
+        for u in range(2):
+            nc.vector.tensor_tensor(out=c_sb[u][:], in0=g_banks[u][:], in1=b_sb[u][:], op=MAX)
+        for t in range(PACK):
+            pick(t == 2, c_pick[:, t, :], c_sb[t // 2][:, (t % 2) * J:(t % 2 + 1) * J], l5)
+
+        hid = sb.tile([P, O * PACK], BF16, name="hid", align_bytes=64)
+        nc.vector.tensor_tensor(
+            out=hid[:].rearrange("p (c i t) -> p c t i", i=4, t=PACK),
+            in0=a_pick[:].rearrange("p t (c i) -> p c t i", i=4),
+            in1=c_pick[:].rearrange("p t (c i) -> p c t i", i=4), op=MAX)
+        hq = sb.tile([P, O], U32, name="hq", align_bytes=64)
+        hs = sb.tile([P, O], U8, name="hs", align_bytes=64)
+        nc.vector.quantize_mx(out=hq[:].bitcast(E5M2), scales=hs[:], in_=hid[:])
+
+        tz_pick = sb.tile([P, 2, O], F32, name="tz_pick")
+        for h in range(2):
+            nc.scalar.activation(out=tz_pick[:, h, :], in_=tzt[h][:].indirect(l6[:]), func=COPY)
+
+        acc = ps.tile([P, 2, O], F32, name="acc")
+        for h in range(2):
+            cols = slice(h * P, (h + 1) * P)
+            nc.tensor.matmul_mx(out=acc[:, h, :], lhsT=wsw[:, cols].bitcast(E4M3), lhsT_scale=wss[:, cols],
+                                rhs=sxw[:].bitcast(E4M3), rhs_scale=sxs[:], start=(h == 0), stop=False)
+        for h in range(2):
+            cols = slice(h * P, (h + 1) * P)
+            nc.tensor.matmul_mx(out=acc[:, h, :], lhsT=wbw[:, cols].bitcast(E2M1), lhsT_scale=wbs[:, cols],
+                                rhs=hq[:].bitcast(E5M2), rhs_scale=hs[:], start=False, stop=(h == 1))
+        y = sb.tile([P, 2, O], F32, name="y")
+        nc.vector.tensor_tensor(out=y[:], in0=acc[:], in1=tz_pick[:], op=ADD)
+        nc.sync.dma_start(out=out.rearrange("(h p) o -> p h o", p=P), in_=y[:])

@@ -24,7 +24,7 @@ PACK = 4
 def load_scales(queue, plane, rows):
     by_row = rows[0].bitcast(I32).rearrange("(q i) c -> i q c", i=4)
     for i in range(4):
-        queue.dma_start(out=plane[:].bitcast(I32)[i:P:32, :], in_=by_row[i])
+        queue.dma_start(out=plane.bitcast(I32)[i:P:32, :], in_=by_row[i])
 
 
 def tile_list_triple_looked_skip_tabled_kernel(
@@ -51,102 +51,103 @@ def tile_list_triple_looked_skip_tabled_kernel(
         wq = sb.tile([P, R], U32, name="wq", align_bytes=64)
         wsc = sb.tile([P, R], U8, name="wsc", align_bytes=64)
         wbw = sb.tile([P, N], U16, name="wbw", align_bytes=64)
-        wbs = sb.tile([P, N], U8, name="wbs", align_bytes=64)
         sxw = sb.tile([P, O], U32, name="sxw", align_bytes=64)
-        sxs = sb.tile([P, O], U8, name="sxs", align_bytes=64)
         wsw = sb.tile([P, N], U32, name="wsw", align_bytes=64)
-        wss = sb.tile([P, N], U8, name="wss", align_bytes=64)
-        tzt = [sb.tile([P, E], F32, name="tz%d" % h) for h in range(2)]
+        late = sb.tile([P, 2 * N + O], U8, name="late", align_bytes=64)
+        wss, wbs, sxs = late[:, 0:N], late[:, N:2 * N], late[:, 2 * N:2 * N + O]
+        tzt = sb.tile([P, 2, E], F32, name="tzt")
 
-        for plane in (wsc_raw, xs, wss, sxs, wbs):
+        for plane in (wsc_raw, xs, late):
             nc.vector.memset(plane[:].bitcast(I32), 0)
-
-        nc.sync.dma_start(lb[:], offs2)
-        load_scales(nc.sync, wsc_raw, w_scales)
-        nc.scalar.dma_start(out=xw[:].bitcast(I32), in_=xt_words[0].bitcast(I32))
-        nc.scalar.dma_start(out=w_raw[:].bitcast(I32), in_=w_words[0].rearrange("p n t -> p (n t)").bitcast(I32))
         nc.sync.dma_start(la[:], offs)
-        load_scales(nc.sync, xs, xt_scales)
+        nc.scalar.dma_start(out=xw[:].bitcast(I32), in_=xt_words[0].bitcast(I32))
+        nc.gpsimd.dma_start(out=w_raw[:].bitcast(I32), in_=w_words[0].rearrange("p n t -> p (n t)").bitcast(I32))
+        load_scales(nc.sync, wsc_raw[:], w_scales)
+        nc.sync.dma_start(lb[:], offs2)
         nc.sync.dma_start(lg[:], offs3)
+        load_scales(nc.sync, xs[:], xt_scales)
         nc.sync.dma_start(l4[:], offs4)
         nc.sync.dma_start(l5[:], offs5)
         nc.sync.dma_start(l6[:], offs6)
-        load_scales(nc.sync, wss, ws_scales)
-        load_scales(nc.sync, sxs, sx_scales)
-        load_scales(nc.sync, wbs, wb_scales)
+        load_scales(nc.gpsimd, wss, ws_scales)
+        load_scales(nc.gpsimd, sxs, sx_scales)
         nc.sync.dma_start(out=wsw[:].bitcast(I32), in_=ws_words[0].rearrange("p n t -> p (n t)").bitcast(I32))
         nc.sync.dma_start(out=sxw[:].bitcast(I32), in_=sx_words[0].rearrange("p n t -> p (n t)").bitcast(I32))
         nc.sync.dma_start(out=wbw[:].bitcast(I32), in_=wb_words[0].bitcast(I32))
-        for h in range(2):
-            nc.sync.dma_start(out=tzt[h][:], in_=tz[h * P:(h + 1) * P, :])
+        load_scales(nc.sync, wbs, wb_scales)
+        nc.sync.dma_start(out=tzt[:], in_=tz.rearrange("(h p) e -> p h e", p=P))
 
         nc.vector.tensor_copy(out=wsc[:].rearrange("p (t m) -> p t m", t=PACK), in_=wsc_raw[:].rearrange("p (m t) -> p t m", t=PACK))
         nc.scalar.copy(out=wq[:].rearrange("p (t m) -> p m t", t=PACK), in_=w_raw[:].rearrange("p (m t) -> p m t", t=PACK))
 
-        def first_stage(name, lst):
-            gw = sb.tile([P, J], U16, name="gw_" + name, align_bytes=64)
-            gs = sb.tile([P, J], U8, name="gs_" + name, align_bytes=64)
-            nc.vector.tensor_copy(out=gw[:], in_=xw[:].indirect(lst[:]))
-            nc.vector.tensor_copy(out=gs[:], in_=xs[:].indirect(lst[:]))
-            banks = []
-            for u in range(2):
-                bank = ps.tile([P, 2 * J], F32, name="bank_%s%d" % (name, u))
-                for v in range(2):
-                    cols = slice((2 * u + v) * P, (2 * u + v + 1) * P)
-                    nc.tensor.matmul_mx(out=bank[:, v * J:(v + 1) * J], lhsT=wq[:, cols].bitcast(E4M3), lhsT_scale=wsc[:, cols],
-                                        rhs=gw[:].bitcast(E2M1), rhs_scale=gs[:], start=True, stop=True)
-                banks.append(bank)
-            return banks
+        names = ("a", "b", "g")
+        gw = [sb.tile([P, J], U16, name="gw_" + s, align_bytes=64) for s in names]
+        gs = [sb.tile([P, J], U8, name="gs_" + s, align_bytes=64) for s in names]
+        for s, lst in enumerate((la, lb, lg)):
+            nc.vector.tensor_copy(out=gw[s][:], in_=xw[:].indirect(lst[:]))
+        for s, lst in enumerate((la, lb, lg)):
+            nc.vector.tensor_copy(out=gs[s][:], in_=xs[:].indirect(lst[:]))
 
-        b_banks = first_stage("b", lb)
-        b_sb = [sb.tile([P, 2 * J], F32, name="b_sb%d" % u) for u in range(2)]
-        for u in range(2):
-            nc.scalar.copy(out=b_sb[u][:], in_=b_banks[u][:])
-        a_banks = first_stage("a", la)
-        a_sb = [sb.tile([P, 2 * J], F32, name="a_sb%d" % u) for u in range(2)]
-        for u in range(2):
-            nc.scalar.copy(out=a_sb[u][:], in_=a_banks[u][:])
-        g_banks = first_stage("g", lg)
+        def product(dst, s, t):
+            cols = slice(t * P, (t + 1) * P)
+            nc.tensor.matmul_mx(out=dst, lhsT=wq[:, cols].bitcast(E4M3), lhsT_scale=wsc[:, cols],
+                                rhs=gw[s][:].bitcast(E2M1), rhs_scale=gs[s][:], start=True, stop=True)
+
+        held = []
+        for s in range(2):
+            for u in range(2):
+                bank = ps.tile([P, 2, J], F32, name="bank%d%d" % (s, u), tag="bank%d%d" % (s, u))
+                for v in range(2):
+                    product(bank[:, v, :], s, 2 * u + v)
+                kept = sb.tile([P, 2, J], F32, name="kept%d%d" % (s, u), tag="kept%d%d" % (s, u))
+                nc.scalar.copy(out=kept[:], in_=bank[:])
+                held.append(kept)
+        a_sb, b_sb = held[:2], held[2:]
 
         a_pick = sb.tile([P, PACK, O], F32, name="a_pick")
         c_pick = sb.tile([P, PACK, O], F32, name="c_pick")
-
-        def pick(on_vector, dst, window, lst):
-            if on_vector:
-                nc.vector.tensor_copy(out=dst, in_=window.indirect(lst[:]))
+        for t in range(PACK):
+            nc.vector.tensor_copy(out=a_pick[:, t, :], in_=a_sb[t // 2][:, t % 2, :].indirect(l4[:]))
+        c_sb = []
+        for t in range(PACK):
+            bank = ps.tile([P, J], F32, name="gbank%d" % t)
+            product(bank[:], 2, t)
+            c1 = sb.tile([P, J], F32, name="c1_%d" % t)
+            nc.vector.tensor_tensor(out=c1[:], in0=bank[:], in1=b_sb[t // 2][:, t % 2, :], op=MAX)
+            c_sb.append(c1)
+        for t in range(PACK):
+            if t < PACK - 1:
+                nc.scalar.activation(out=c_pick[:, t, :], in_=c_sb[t][:].indirect(l5[:]), func=COPY)
             else:
-                nc.scalar.activation(out=dst, in_=window.indirect(lst[:]), func=COPY)
-
-        for t in range(PACK):
-            pick(t < 2, a_pick[:, t, :], a_sb[t // 2][:, (t % 2) * J:(t % 2 + 1) * J], l4)
-        c_sb = [sb.tile([P, 2 * J], F32, name="c_sb%d" % u) for u in range(2)]
-        for u in range(2):
-            nc.vector.tensor_tensor(out=c_sb[u][:], in0=g_banks[u][:], in1=b_sb[u][:], op=MAX)
-        for t in range(PACK):
-            pick(t == 2, c_pick[:, t, :], c_sb[t // 2][:, (t % 2) * J:(t % 2 + 1) * J], l5)
+                nc.vector.tensor_copy(out=c_pick[:, t, :], in_=c_sb[t][:].indirect(l5[:]))
 
         hid = sb.tile([P, O * PACK], BF16, name="hid", align_bytes=64)
-        nc.vector.tensor_tensor(
-            out=hid[:].rearrange("p (c i t) -> p c t i", i=4, t=PACK),
-            in0=a_pick[:].rearrange("p t (c i) -> p c t i", i=4),
-            in1=c_pick[:].rearrange("p t (c i) -> p c t i", i=4), op=MAX)
         hq = sb.tile([P, O], U32, name="hq", align_bytes=64)
         hs = sb.tile([P, O], U8, name="hs", align_bytes=64)
-        nc.vector.quantize_mx(out=hq[:].bitcast(E5M2), scales=hs[:], in_=hid[:])
+        half = O // 2
+        for u in range(2):
+            cols = slice(u * half, (u + 1) * half)
+            nc.vector.tensor_tensor(
+                out=hid[:, u * half * PACK:(u + 1) * half * PACK].rearrange("p (c i t) -> p c t i", i=4, t=PACK),
+                in0=a_pick[:, :, cols].rearrange("p t (c i) -> p c t i", i=4),
+                in1=c_pick[:, :, cols].rearrange("p t (c i) -> p c t i", i=4), op=MAX)
+        for u in range(2):
+            cols = slice(u * half, (u + 1) * half)
+            nc.vector.quantize_mx(out=hq[:, cols].bitcast(E5M2), scales=hs[:, cols], in_=hid[:, u * half * PACK:(u + 1) * half * PACK])
 
-        tz_pick = sb.tile([P, 2, O], F32, name="tz_pick")
+        tz_pick = sb.tile([P, 2, O], F32, name="tz_pick", tag="kept11")
         for h in range(2):
-            nc.scalar.activation(out=tz_pick[:, h, :], in_=tzt[h][:].indirect(l6[:]), func=COPY)
+            nc.scalar.activation(out=tz_pick[:, h, :], in_=tzt[:, h, :].indirect(l6[:]), func=COPY)
 
-        acc = ps.tile([P, 2, O], F32, name="acc")
+        acc = [ps.tile([P, O], F32, name="acc%d" % h, tag="bank0%d" % h) for h in range(2)]
         for h in range(2):
             cols = slice(h * P, (h + 1) * P)
-            nc.tensor.matmul_mx(out=acc[:, h, :], lhsT=wsw[:, cols].bitcast(E4M3), lhsT_scale=wss[:, cols],
-                                rhs=sxw[:].bitcast(E4M3), rhs_scale=sxs[:], start=(h == 0), stop=False)
+            nc.tensor.matmul_mx(out=acc[h][:], lhsT=wsw[:, cols].bitcast(E4M3), lhsT_scale=wss[:, cols],
+                                rhs=sxw[:].bitcast(E4M3), rhs_scale=sxs, start=True, stop=False)
         for h in range(2):
             cols = slice(h * P, (h + 1) * P)
-            nc.tensor.matmul_mx(out=acc[:, h, :], lhsT=wbw[:, cols].bitcast(E2M1), lhsT_scale=wbs[:, cols],
-                                rhs=hq[:].bitcast(E5M2), rhs_scale=hs[:], start=False, stop=(h == 1))
-        y = sb.tile([P, 2, O], F32, name="y")
-        nc.vector.tensor_tensor(out=y[:], in0=acc[:], in1=tz_pick[:], op=ADD)
-        nc.sync.dma_start(out=out.rearrange("(h p) o -> p h o", p=P), in_=y[:])
+            nc.tensor.matmul_mx(out=acc[h][:], lhsT=wbw[:, cols].bitcast(E2M1), lhsT_scale=wbs[:, cols],
+                                rhs=hq[:].bitcast(E5M2), rhs_scale=hs[:], start=False, stop=True)
+            y = sb.tile([P, O], F32, name="y%d" % h)
+            nc.vector.tensor_tensor(out=y[:], in0=acc[h][:], in1=tz_pick[:, h, :], op=ADD)
+            (nc.sync, nc.scalar)[h].dma_start(out=out[cols, :], in_=y[:])

@@ -21,9 +21,9 @@ P = 128
 PACK = 4
 
 
-def load_scales(queue, plane, rows):
+def load_scales(queue, plane, rows, which=range(4)):
     by_row = rows[0].bitcast(I32).rearrange("(q i) c -> i q c", i=4)
-    for i in range(4):
+    for i in which:
         queue.dma_start(out=plane.bitcast(I32)[i:P:32, :], in_=by_row[i])
 
 
@@ -57,35 +57,38 @@ def tile_list_triple_looked_skip_tabled_kernel(
         wss, wbs, sxs = late[:, 0:N], late[:, N:2 * N], late[:, 2 * N:2 * N + O]
         tzt = sb.tile([P, 2, E], F32, name="tzt")
 
-        for plane in (wsc_raw, xs, late):
+        for plane in (wsc_raw, xs):
             nc.vector.memset(plane[:].bitcast(I32), 0)
+        nc.gpsimd.memset(late[:].bitcast(I32), 0)
         nc.sync.dma_start(la[:], offs)
-        nc.scalar.dma_start(out=xw[:].bitcast(I32), in_=xt_words[0].bitcast(I32))
-        nc.gpsimd.dma_start(out=w_raw[:].bitcast(I32), in_=w_words[0].rearrange("p n t -> p (n t)").bitcast(I32))
-        load_scales(nc.sync, wsc_raw[:], w_scales)
-        nc.sync.dma_start(lb[:], offs2)
-        nc.sync.dma_start(lg[:], offs3)
-        load_scales(nc.sync, xs[:], xt_scales)
         nc.sync.dma_start(l4[:], offs4)
         nc.sync.dma_start(l5[:], offs5)
+        load_scales(nc.sync, wsc_raw[:], w_scales, (0, 2))
+        load_scales(nc.scalar, wsc_raw[:], w_scales, (1, 3))
+        nc.sync.dma_start(out=xw[:].bitcast(I32), in_=xt_words[0].bitcast(I32))
+        load_scales(nc.sync, xs[:], xt_scales)
+        nc.sync.dma_start(out=w_raw[:].bitcast(I32), in_=w_words[0].rearrange("p n t -> p (n t)").bitcast(I32))
+        nc.sync.dma_start(lb[:], offs2)
+        nc.sync.dma_start(lg[:], offs3)
+        nc.sync.dma_start(out=tzt[:], in_=tz.rearrange("(h p) e -> p h e", p=P))
+        load_scales(nc.sync, wss, ws_scales)
+        load_scales(nc.sync, sxs, sx_scales)
         nc.sync.dma_start(l6[:], offs6)
-        load_scales(nc.gpsimd, wss, ws_scales)
-        load_scales(nc.gpsimd, sxs, sx_scales)
-        nc.sync.dma_start(out=wsw[:].bitcast(I32), in_=ws_words[0].rearrange("p n t -> p (n t)").bitcast(I32))
         nc.sync.dma_start(out=sxw[:].bitcast(I32), in_=sx_words[0].rearrange("p n t -> p (n t)").bitcast(I32))
+        nc.sync.dma_start(out=wsw[:].bitcast(I32), in_=ws_words[0].rearrange("p n t -> p (n t)").bitcast(I32))
         nc.sync.dma_start(out=wbw[:].bitcast(I32), in_=wb_words[0].bitcast(I32))
         load_scales(nc.sync, wbs, wb_scales)
-        nc.sync.dma_start(out=tzt[:], in_=tz.rearrange("(h p) e -> p h e", p=P))
 
         nc.vector.tensor_copy(out=wsc[:].rearrange("p (t m) -> p t m", t=PACK), in_=wsc_raw[:].rearrange("p (m t) -> p t m", t=PACK))
-        nc.scalar.copy(out=wq[:].rearrange("p (t m) -> p m t", t=PACK), in_=w_raw[:].rearrange("p (m t) -> p m t", t=PACK))
+        for u in range(2):
+            nc.scalar.copy(out=wq[:, u * 2 * P:(u + 1) * 2 * P].rearrange("p (t m) -> p m t", t=2),
+                           in_=w_raw[:].rearrange("p (m t) -> p m t", t=PACK)[:, :, 2 * u:2 * u + 2])
 
         names = ("a", "b", "g")
         gw = [sb.tile([P, J], U16, name="gw_" + s, align_bytes=64) for s in names]
         gs = [sb.tile([P, J], U8, name="gs_" + s, align_bytes=64) for s in names]
         for s, lst in enumerate((la, lb, lg)):
             nc.vector.tensor_copy(out=gw[s][:], in_=xw[:].indirect(lst[:]))
-        for s, lst in enumerate((la, lb, lg)):
             nc.vector.tensor_copy(out=gs[s][:], in_=xs[:].indirect(lst[:]))
 
         def product(dst, s, t):
@@ -93,24 +96,32 @@ def tile_list_triple_looked_skip_tabled_kernel(
             nc.tensor.matmul_mx(out=dst, lhsT=wq[:, cols].bitcast(E4M3), lhsT_scale=wsc[:, cols],
                                 rhs=gw[s][:].bitcast(E2M1), rhs_scale=gs[s][:], start=True, stop=True)
 
-        held = []
-        for s in range(2):
-            for u in range(2):
-                bank = ps.tile([P, 2, J], F32, name="bank%d%d" % (s, u), tag="bank%d%d" % (s, u))
-                for v in range(2):
-                    product(bank[:, v, :], s, 2 * u + v)
-                kept = sb.tile([P, 2, J], F32, name="kept%d%d" % (s, u), tag="kept%d%d" % (s, u))
-                nc.scalar.copy(out=kept[:], in_=bank[:])
-                held.append(kept)
-        a_sb, b_sb = held[:2], held[2:]
+        a_sb = []
+        for t in range(PACK):
+            bank = ps.tile([P, J], F32, name="abank%d" % t, tag="bank%d" % t)
+            product(bank[:], 0, t)
+            kept = sb.tile([P, J], F32, name="a_sb%d" % t)
+            nc.scalar.copy(out=kept[:], in_=bank[:])
+            a_sb.append(kept)
+        b_sb = []
+        for u in range(2):
+            bank = ps.tile([P, 2, J], F32, name="bbank%d" % u)
+            for v in range(2):
+                product(bank[:, v, :], 1, 2 * u + v)
+            kept = sb.tile([P, 2, J], F32, name="b_sb%d" % u, tag="kept1%d" % u)
+            nc.scalar.copy(out=kept[:], in_=bank[:])
+            b_sb.append(kept)
 
         a_pick = sb.tile([P, PACK, O], F32, name="a_pick")
         c_pick = sb.tile([P, PACK, O], F32, name="c_pick")
         for t in range(PACK):
-            nc.vector.tensor_copy(out=a_pick[:, t, :], in_=a_sb[t // 2][:, t % 2, :].indirect(l4[:]))
+            if t < 2:
+                nc.scalar.activation(out=a_pick[:, t, :], in_=a_sb[t][:].indirect(l4[:]), func=COPY)
+            else:
+                nc.vector.tensor_copy(out=a_pick[:, t, :], in_=a_sb[t][:].indirect(l4[:]))
         c_sb = []
         for t in range(PACK):
-            bank = ps.tile([P, J], F32, name="gbank%d" % t)
+            bank = ps.tile([P, J], F32, name="gbank%d" % t, tag="bank%d" % t)
             product(bank[:], 2, t)
             c1 = sb.tile([P, J], F32, name="c1_%d" % t)
             nc.vector.tensor_tensor(out=c1[:], in0=bank[:], in1=b_sb[t // 2][:, t % 2, :], op=MAX)
@@ -139,7 +150,7 @@ def tile_list_triple_looked_skip_tabled_kernel(
         for h in range(2):
             nc.scalar.activation(out=tz_pick[:, h, :], in_=tzt[:, h, :].indirect(l6[:]), func=COPY)
 
-        acc = [ps.tile([P, O], F32, name="acc%d" % h, tag="bank0%d" % h) for h in range(2)]
+        acc = [ps.tile([P, O], F32, name="acc%d" % h) for h in range(2)]
         for h in range(2):
             cols = slice(h * P, (h + 1) * P)
             nc.tensor.matmul_mx(out=acc[h][:], lhsT=wsw[:, cols].bitcast(E4M3), lhsT_scale=wss[:, cols],

@@ -17,14 +17,31 @@ E2M1 = mybir.dt.float4_e2m1fn_x4
 COPY = mybir.ActivationFunctionType.Copy
 MAX = mybir.AluOpType.max
 ADD = mybir.AluOpType.add
+
 P = 128
 PACK = 4
+QUADRANT = 32
+GROUP = 16
+MX_ALIGN = 64
+A_PICKS_ON_SCALAR = 1
+C_PICKS_ON_SCALAR = 3
 
 
-def load_scales(queue, plane, rows, which=range(4)):
-    by_row = rows[0].bitcast(I32).rearrange("(q i) c -> i q c", i=4)
-    for i in which:
-        queue.dma_start(out=plane.bitcast(I32)[i:P:32, :], in_=by_row[i])
+def load_scale_rows(queue, plane, scales, places=range(PACK)):
+    by_place = scales[0].bitcast(I32).rearrange("(q i) c -> i q c", i=PACK)
+    for i in places:
+        queue.dma_start(out=plane.bitcast(I32)[i:P:QUADRANT, :], in_=by_place[i])
+
+
+def fp8_words(words):
+    return words[0].rearrange("p n t -> p (n t)").bitcast(I32)
+
+
+def pick(nc, on_scalar, picked, window, entries):
+    if on_scalar:
+        nc.scalar.activation(out=picked, in_=window.indirect(entries), func=COPY)
+    else:
+        nc.vector.tensor_copy(out=picked, in_=window.indirect(entries))
 
 
 def tile_list_triple_looked_skip_tabled_kernel(
@@ -37,128 +54,127 @@ def tile_list_triple_looked_skip_tabled_kernel(
         sb = ctx.enter_context(tc.tile_pool(name="sb", bufs=1))
         ps = ctx.enter_context(tc.psum_pool(name="ps", bufs=1))
 
-        la = lists.tile([P, J // 16], U16, name="la")
-        lb = lists.tile([P, J // 16], U16, name="lb")
-        lg = lists.tile([P, J // 16], U16, name="lg")
-        l4 = lists.tile([P, O // 16], U16, name="l4")
-        l5 = lists.tile([P, O // 16], U16, name="l5")
-        l6 = lists.tile([P, O // 16], U16, name="l6")
+        list_a = lists.tile([P, J // GROUP], U16, name="list_a")
+        list_b = lists.tile([P, J // GROUP], U16, name="list_b")
+        list_g = lists.tile([P, J // GROUP], U16, name="list_g")
+        list_of_a = lists.tile([P, O // GROUP], U16, name="list_of_a")
+        list_of_c = lists.tile([P, O // GROUP], U16, name="list_of_c")
+        list_of_tz = lists.tile([P, O // GROUP], U16, name="list_of_tz")
 
-        xw = sb.tile([P, T], U16, name="xw", align_bytes=64)
-        xs = sb.tile([P, T], U8, name="xs", align_bytes=64)
-        w_raw = sb.tile([P, R], U32, name="w_raw", align_bytes=64)
-        wsc_raw = sb.tile([P, R], U8, name="wsc_raw", align_bytes=64)
-        wq = sb.tile([P, R], U32, name="wq", align_bytes=64)
-        wsc = sb.tile([P, R], U8, name="wsc", align_bytes=64)
-        wbw = sb.tile([P, N], U16, name="wbw", align_bytes=64)
-        sxw = sb.tile([P, O], U32, name="sxw", align_bytes=64)
-        wsw = sb.tile([P, N], U32, name="wsw", align_bytes=64)
-        late = sb.tile([P, 2 * N + O], U8, name="late", align_bytes=64)
-        wss, wbs, sxs = late[:, 0:N], late[:, N:2 * N], late[:, 2 * N:2 * N + O]
-        tzt = sb.tile([P, 2, E], F32, name="tzt")
+        xt_w = sb.tile([P, T], U16, name="xt_w", align_bytes=MX_ALIGN)
+        xt_s = sb.tile([P, T], U8, name="xt_s", align_bytes=MX_ALIGN)
+        w_w_given = sb.tile([P, R], U32, name="w_w_given", align_bytes=MX_ALIGN)
+        w_s_given = sb.tile([P, R], U8, name="w_s_given", align_bytes=MX_ALIGN)
+        w_w = sb.tile([P, R], U32, name="w_w", align_bytes=MX_ALIGN)
+        w_s = sb.tile([P, R], U8, name="w_s", align_bytes=MX_ALIGN)
+        wb_w = sb.tile([P, N], U16, name="wb_w", align_bytes=MX_ALIGN)
+        sx_w = sb.tile([P, O], U32, name="sx_w", align_bytes=MX_ALIGN)
+        ws_w = sb.tile([P, N], U32, name="ws_w", align_bytes=MX_ALIGN)
+        out_stage_s = sb.tile([P, 2 * N + O], U8, name="out_stage_s", align_bytes=MX_ALIGN)
+        ws_s, wb_s, sx_s = out_stage_s[:, 0:N], out_stage_s[:, N:2 * N], out_stage_s[:, 2 * N:2 * N + O]
+        tz_rows = [sb.tile([P, E], F32, name="tz_rows%d" % h) for h in range(N // P)]
 
-        for plane in (wsc_raw, xs):
+        for plane in (w_s_given, xt_s, out_stage_s):
             nc.vector.memset(plane[:].bitcast(I32), 0)
-        nc.gpsimd.memset(late[:].bitcast(I32), 0)
-        nc.sync.dma_start(la[:], offs)
-        nc.sync.dma_start(l4[:], offs4)
-        nc.sync.dma_start(l5[:], offs5)
-        load_scales(nc.sync, wsc_raw[:], w_scales, (0, 2))
-        load_scales(nc.scalar, wsc_raw[:], w_scales, (1, 3))
-        nc.sync.dma_start(out=xw[:].bitcast(I32), in_=xt_words[0].bitcast(I32))
-        load_scales(nc.sync, xs[:], xt_scales)
-        nc.sync.dma_start(out=w_raw[:].bitcast(I32), in_=w_words[0].rearrange("p n t -> p (n t)").bitcast(I32))
-        nc.sync.dma_start(lb[:], offs2)
-        nc.sync.dma_start(lg[:], offs3)
-        nc.sync.dma_start(out=tzt[:], in_=tz.rearrange("(h p) e -> p h e", p=P))
-        load_scales(nc.sync, wss, ws_scales)
-        load_scales(nc.sync, sxs, sx_scales)
-        nc.sync.dma_start(l6[:], offs6)
-        nc.sync.dma_start(out=sxw[:].bitcast(I32), in_=sx_words[0].rearrange("p n t -> p (n t)").bitcast(I32))
-        nc.sync.dma_start(out=wsw[:].bitcast(I32), in_=ws_words[0].rearrange("p n t -> p (n t)").bitcast(I32))
-        nc.sync.dma_start(out=wbw[:].bitcast(I32), in_=wb_words[0].bitcast(I32))
-        load_scales(nc.sync, wbs, wb_scales)
 
-        nc.vector.tensor_copy(out=wsc[:].rearrange("p (t m) -> p t m", t=PACK), in_=wsc_raw[:].rearrange("p (m t) -> p t m", t=PACK))
-        for u in range(2):
-            nc.scalar.copy(out=wq[:, u * 2 * P:(u + 1) * 2 * P].rearrange("p (t m) -> p m t", t=2),
-                           in_=w_raw[:].rearrange("p (m t) -> p m t", t=PACK)[:, :, 2 * u:2 * u + 2])
+        nc.sync.dma_start(list_a[:], offs)
+        nc.sync.dma_start(list_of_a[:], offs4)
+        nc.sync.dma_start(list_of_c[:], offs5)
+        load_scale_rows(nc.sync, w_s_given[:], w_scales, (0, 2))
+        load_scale_rows(nc.scalar, w_s_given[:], w_scales, (1, 3))
+        nc.sync.dma_start(out=xt_w[:].bitcast(I32), in_=xt_words[0].bitcast(I32))
+        load_scale_rows(nc.sync, xt_s[:], xt_scales)
+        nc.sync.dma_start(list_b[:], offs2)
+        nc.sync.dma_start(out=w_w_given[:].bitcast(I32), in_=fp8_words(w_words))
+        nc.sync.dma_start(list_g[:], offs3)
+        nc.sync.dma_start(out=tz_rows[0][:], in_=tz[0:P, :])
+        load_scale_rows(nc.gpsimd, sx_s, sx_scales, (0, 1))
+        load_scale_rows(nc.sync, sx_s, sx_scales, (2, 3))
+        load_scale_rows(nc.sync, ws_s, ws_scales)
+        load_scale_rows(nc.sync, wb_s, wb_scales, (0,))
+        nc.sync.dma_start(out=tz_rows[1][:], in_=tz[P:2 * P, :])
+        load_scale_rows(nc.sync, wb_s, wb_scales, (1, 2, 3))
+        nc.sync.dma_start(list_of_tz[:], offs6)
+        nc.sync.dma_start(out=sx_w[:].bitcast(I32), in_=fp8_words(sx_words))
+        nc.sync.dma_start(out=ws_w[:].bitcast(I32), in_=fp8_words(ws_words))
+        nc.sync.dma_start(out=wb_w[:].bitcast(I32), in_=wb_words[0].bitcast(I32))
+
+        nc.vector.tensor_copy(out=w_s[:].rearrange("p (t m) -> p t m", t=PACK),
+                              in_=w_s_given[:].rearrange("p (m t) -> p t m", t=PACK))
+        for u in range(PACK // 2):
+            nc.scalar.copy(out=w_w[:, u * 2 * P:(u + 1) * 2 * P].rearrange("p (t m) -> p m t", t=2),
+                           in_=w_w_given[:].rearrange("p (m t) -> p m t", t=PACK)[:, :, 2 * u:2 * u + 2])
 
         names = ("a", "b", "g")
-        gw = [sb.tile([P, J], U16, name="gw_" + s, align_bytes=64) for s in names]
-        gs = [sb.tile([P, J], U8, name="gs_" + s, align_bytes=64) for s in names]
-        for s, lst in enumerate((la, lb, lg)):
-            nc.vector.tensor_copy(out=gw[s][:], in_=xw[:].indirect(lst[:]))
-            nc.vector.tensor_copy(out=gs[s][:], in_=xs[:].indirect(lst[:]))
+        tok_w = [sb.tile([P, J], U16, name="tok_w_" + s, align_bytes=MX_ALIGN) for s in names]
+        tok_s = [sb.tile([P, J], U8, name="tok_s_" + s, align_bytes=MX_ALIGN) for s in names]
+        for s, entries in enumerate((list_a, list_b, list_g)):
+            nc.vector.tensor_copy(out=tok_w[s][:], in_=xt_w[:].indirect(entries[:]))
+            nc.vector.tensor_copy(out=tok_s[s][:], in_=xt_s[:].indirect(entries[:]))
 
-        def product(dst, s, t):
+        def first_stage(result, s, t):
             cols = slice(t * P, (t + 1) * P)
-            nc.tensor.matmul_mx(out=dst, lhsT=wq[:, cols].bitcast(E4M3), lhsT_scale=wsc[:, cols],
-                                rhs=gw[s][:].bitcast(E2M1), rhs_scale=gs[s][:], start=True, stop=True)
+            nc.tensor.matmul_mx(out=result, lhsT=w_w[:, cols].bitcast(E4M3), lhsT_scale=w_s[:, cols],
+                                rhs=tok_w[s][:].bitcast(E2M1), rhs_scale=tok_s[s][:], start=True, stop=True)
 
-        a_sb = []
+        a_slices = []
         for t in range(PACK):
-            bank = ps.tile([P, J], F32, name="abank%d" % t, tag="bank%d" % t)
-            product(bank[:], 0, t)
-            kept = sb.tile([P, J], F32, name="a_sb%d" % t)
-            nc.scalar.copy(out=kept[:], in_=bank[:])
-            a_sb.append(kept)
-        b_sb = []
-        for u in range(2):
-            bank = ps.tile([P, 2, J], F32, name="bbank%d" % u)
+            bank = ps.tile([P, J], F32, name="a_bank%d" % t, tag="slice_bank%d" % t)
+            first_stage(bank[:], 0, t)
+            a_slice = sb.tile([P, J], F32, name="a_slice%d" % t)
+            nc.scalar.copy(out=a_slice[:], in_=bank[:])
+            a_slices.append(a_slice)
+        b_pairs = []
+        for u in range(PACK // 2):
+            bank = ps.tile([P, 2, J], F32, name="b_bank%d" % u)
             for v in range(2):
-                product(bank[:, v, :], 1, 2 * u + v)
-            kept = sb.tile([P, 2, J], F32, name="b_sb%d" % u, tag="kept1%d" % u)
-            nc.scalar.copy(out=kept[:], in_=bank[:])
-            b_sb.append(kept)
+                first_stage(bank[:, v, :], 1, 2 * u + v)
+            b_pair = sb.tile([P, 2, J], F32, name="b_pair%d" % u, tag="b_pair%d" % u)
+            nc.scalar.copy(out=b_pair[:], in_=bank[:])
+            b_pairs.append(b_pair)
 
-        a_pick = sb.tile([P, PACK, O], F32, name="a_pick")
-        c_pick = sb.tile([P, PACK, O], F32, name="c_pick")
+        a_picked = sb.tile([P, PACK, O], F32, name="a_picked")
+        c_picked = sb.tile([P, PACK, O], F32, name="c_picked")
         for t in range(PACK):
-            if t < 2:
-                nc.scalar.activation(out=a_pick[:, t, :], in_=a_sb[t][:].indirect(l4[:]), func=COPY)
-            else:
-                nc.vector.tensor_copy(out=a_pick[:, t, :], in_=a_sb[t][:].indirect(l4[:]))
-        c_sb = []
+            pick(nc, t < A_PICKS_ON_SCALAR, a_picked[:, t, :], a_slices[t][:], list_of_a[:])
+        c_slices = []
         for t in range(PACK):
-            bank = ps.tile([P, J], F32, name="gbank%d" % t, tag="bank%d" % t)
-            product(bank[:], 2, t)
-            c1 = sb.tile([P, J], F32, name="c1_%d" % t)
-            nc.vector.tensor_tensor(out=c1[:], in0=bank[:], in1=b_sb[t // 2][:, t % 2, :], op=MAX)
-            c_sb.append(c1)
+            bank = ps.tile([P, J], F32, name="g_bank%d" % t, tag="slice_bank%d" % t)
+            first_stage(bank[:], 2, t)
+            c_slice = sb.tile([P, J], F32, name="c_slice%d" % t)
+            nc.vector.tensor_tensor(out=c_slice[:], in0=bank[:], in1=b_pairs[t // 2][:, t % 2, :], op=MAX)
+            c_slices.append(c_slice)
         for t in range(PACK):
-            if t < PACK - 1:
-                nc.scalar.activation(out=c_pick[:, t, :], in_=c_sb[t][:].indirect(l5[:]), func=COPY)
-            else:
-                nc.vector.tensor_copy(out=c_pick[:, t, :], in_=c_sb[t][:].indirect(l5[:]))
+            pick(nc, t < C_PICKS_ON_SCALAR, c_picked[:, t, :], c_slices[t][:], list_of_c[:])
 
-        hid = sb.tile([P, O * PACK], BF16, name="hid", align_bytes=64)
-        hq = sb.tile([P, O], U32, name="hq", align_bytes=64)
-        hs = sb.tile([P, O], U8, name="hs", align_bytes=64)
+        hid = sb.tile([P, O * PACK], BF16, name="hid", align_bytes=MX_ALIGN)
+        hid_w = sb.tile([P, O], U32, name="hid_w", align_bytes=MX_ALIGN)
+        hid_s = sb.tile([P, O], U8, name="hid_s", align_bytes=MX_ALIGN)
         half = O // 2
         for u in range(2):
-            cols = slice(u * half, (u + 1) * half)
+            places = slice(u * half, (u + 1) * half)
             nc.vector.tensor_tensor(
                 out=hid[:, u * half * PACK:(u + 1) * half * PACK].rearrange("p (c i t) -> p c t i", i=4, t=PACK),
-                in0=a_pick[:, :, cols].rearrange("p t (c i) -> p c t i", i=4),
-                in1=c_pick[:, :, cols].rearrange("p t (c i) -> p c t i", i=4), op=MAX)
+                in0=a_picked[:, :, places].rearrange("p t (c i) -> p c t i", i=4),
+                in1=c_picked[:, :, places].rearrange("p t (c i) -> p c t i", i=4), op=MAX)
         for u in range(2):
-            cols = slice(u * half, (u + 1) * half)
-            nc.vector.quantize_mx(out=hq[:, cols].bitcast(E5M2), scales=hs[:, cols], in_=hid[:, u * half * PACK:(u + 1) * half * PACK])
+            places = slice(u * half, (u + 1) * half)
+            nc.vector.quantize_mx(out=hid_w[:, places].bitcast(E5M2), scales=hid_s[:, places],
+                                  in_=hid[:, u * half * PACK:(u + 1) * half * PACK])
 
-        tz_pick = sb.tile([P, 2, O], F32, name="tz_pick", tag="kept11")
-        for h in range(2):
-            nc.scalar.activation(out=tz_pick[:, h, :], in_=tzt[:, h, :].indirect(l6[:]), func=COPY)
+        tz_picked = sb.tile([P, N // P, O], F32, name="tz_picked", tag="b_pair1")
+        for h in range(N // P):
+            pick(nc, True, tz_picked[:, h, :], tz_rows[h][:], list_of_tz[:])
 
-        acc = [ps.tile([P, O], F32, name="acc%d" % h) for h in range(2)]
-        for h in range(2):
+        sums = [ps.tile([P, O], F32, name="sum%d" % h) for h in range(N // P)]
+        for h in range(N // P):
             cols = slice(h * P, (h + 1) * P)
-            nc.tensor.matmul_mx(out=acc[h][:], lhsT=wsw[:, cols].bitcast(E4M3), lhsT_scale=wss[:, cols],
-                                rhs=sxw[:].bitcast(E4M3), rhs_scale=sxs, start=True, stop=False)
-        for h in range(2):
+            nc.tensor.matmul_mx(out=sums[h][:], lhsT=ws_w[:, cols].bitcast(E4M3), lhsT_scale=ws_s[:, cols],
+                                rhs=sx_w[:].bitcast(E4M3), rhs_scale=sx_s, start=True, stop=False)
+        for h in range(N // P):
             cols = slice(h * P, (h + 1) * P)
-            nc.tensor.matmul_mx(out=acc[h][:], lhsT=wbw[:, cols].bitcast(E2M1), lhsT_scale=wbs[:, cols],
-                                rhs=hq[:].bitcast(E5M2), rhs_scale=hs[:], start=False, stop=True)
-            y = sb.tile([P, O], F32, name="y%d" % h)
-            nc.vector.tensor_tensor(out=y[:], in0=acc[h][:], in1=tz_pick[:, h, :], op=ADD)
-            (nc.sync, nc.scalar)[h].dma_start(out=out[cols, :], in_=y[:])
+            nc.tensor.matmul_mx(out=sums[h][:], lhsT=wb_w[:, cols].bitcast(E2M1), lhsT_scale=wb_s[:, cols],
+                                rhs=hid_w[:].bitcast(E5M2), rhs_scale=hid_s[:], start=False, stop=True)
+            result = sb.tile([P, O], F32, name="result%d" % h)
+            nc.vector.tensor_tensor(out=result[:], in0=sums[h][:], in1=tz_picked[:, h, :], op=ADD)
+            (nc.sync, nc.scalar)[h].dma_start(out=out[cols, :], in_=result[:])

from contextlib import ExitStack

import concourse.mybir as mybir

K, T, J, R, O, N, L, E = 512, 2048, 256, 512, 128, 256, 512, 1024
FLOPS = 2 * (3 * K * R * J + R * N * O + L * N * O)

F32 = mybir.dt.float32
BF16 = mybir.dt.bfloat16
I32 = mybir.dt.int32
U32 = mybir.dt.uint32
U16 = mybir.dt.uint16
U8 = mybir.dt.uint8
E4M3 = mybir.dt.float8_e4m3fn_x4
E5M2 = mybir.dt.float8_e5m2_x4
E2M1 = mybir.dt.float4_e2m1fn_x4
COPY = mybir.ActivationFunctionType.Copy
MAX = mybir.AluOpType.max
ADD = mybir.AluOpType.add

P = 128
PACK = 4
QUADRANT = 32
GROUP = 16
MX_ALIGN = 64
A_PICKS_ON_SCALAR = 1
C_PICKS_ON_SCALAR = 3


def load_scale_rows(queue, plane, scales, places=range(PACK)):
    by_place = scales[0].bitcast(I32).rearrange("(q i) c -> i q c", i=PACK)
    for i in places:
        queue.dma_start(out=plane.bitcast(I32)[i:P:QUADRANT, :], in_=by_place[i])


def fp8_words(words):
    return words[0].rearrange("p n t -> p (n t)").bitcast(I32)


def pick(nc, on_scalar, picked, window, entries):
    if on_scalar:
        nc.scalar.activation(out=picked, in_=window.indirect(entries), func=COPY)
    else:
        nc.vector.tensor_copy(out=picked, in_=window.indirect(entries))


def tile_list_triple_looked_skip_tabled_kernel(
    tc, xt_words, xt_scales, w_words, w_scales, wb_words, wb_scales, sx_words, sx_scales,
    ws_words, ws_scales, tz, offs, offs2, offs3, offs4, offs5, offs6, out,
):
    nc = tc.nc
    with ExitStack() as ctx:
        lists = ctx.enter_context(tc.tile_pool(name="lists", bufs=1))
        sb = ctx.enter_context(tc.tile_pool(name="sb", bufs=1))
        ps = ctx.enter_context(tc.psum_pool(name="ps", bufs=1))

        list_a = lists.tile([P, J // GROUP], U16, name="list_a")
        list_b = lists.tile([P, J // GROUP], U16, name="list_b")
        list_g = lists.tile([P, J // GROUP], U16, name="list_g")
        list_of_a = lists.tile([P, O // GROUP], U16, name="list_of_a")
        list_of_c = lists.tile([P, O // GROUP], U16, name="list_of_c")
        list_of_tz = lists.tile([P, O // GROUP], U16, name="list_of_tz")

        xt_w = sb.tile([P, T], U16, name="xt_w", align_bytes=MX_ALIGN)
        xt_s = sb.tile([P, T], U8, name="xt_s", align_bytes=MX_ALIGN)
        w_w_given = sb.tile([P, R], U32, name="w_w_given", align_bytes=MX_ALIGN)
        w_s_given = sb.tile([P, R], U8, name="w_s_given", align_bytes=MX_ALIGN)
        w_w = sb.tile([P, R], U32, name="w_w", align_bytes=MX_ALIGN)
        w_s = sb.tile([P, R], U8, name="w_s", align_bytes=MX_ALIGN)
        wb_w = sb.tile([P, N], U16, name="wb_w", align_bytes=MX_ALIGN)
        sx_w = sb.tile([P, O], U32, name="sx_w", align_bytes=MX_ALIGN)
        ws_w = sb.tile([P, N], U32, name="ws_w", align_bytes=MX_ALIGN)
        out_stage_s = sb.tile([P, 2 * N + O], U8, name="out_stage_s", align_bytes=MX_ALIGN)
        ws_s, wb_s, sx_s = out_stage_s[:, 0:N], out_stage_s[:, N:2 * N], out_stage_s[:, 2 * N:2 * N + O]
        tz_rows = [sb.tile([P, E], F32, name="tz_rows%d" % h) for h in range(N // P)]

        for plane in (w_s_given, xt_s, out_stage_s):
            nc.vector.memset(plane[:].bitcast(I32), 0)

        nc.sync.dma_start(list_a[:], offs)
        nc.sync.dma_start(list_of_a[:], offs4)
        nc.sync.dma_start(list_of_c[:], offs5)
        load_scale_rows(nc.sync, w_s_given[:], w_scales, (0, 2))
        load_scale_rows(nc.scalar, w_s_given[:], w_scales, (1, 3))
        nc.sync.dma_start(out=xt_w[:].bitcast(I32), in_=xt_words[0].bitcast(I32))
        load_scale_rows(nc.sync, xt_s[:], xt_scales)
        nc.sync.dma_start(list_b[:], offs2)
        nc.sync.dma_start(out=w_w_given[:].bitcast(I32), in_=fp8_words(w_words))
        nc.sync.dma_start(list_g[:], offs3)
        nc.sync.dma_start(out=tz_rows[0][:], in_=tz[0:P, :])
        load_scale_rows(nc.gpsimd, sx_s, sx_scales, (0, 1))
        load_scale_rows(nc.sync, sx_s, sx_scales, (2, 3))
        load_scale_rows(nc.sync, ws_s, ws_scales)
        load_scale_rows(nc.sync, wb_s, wb_scales, (0,))
        nc.sync.dma_start(out=tz_rows[1][:], in_=tz[P:2 * P, :])
        load_scale_rows(nc.sync, wb_s, wb_scales, (1, 2, 3))
        nc.sync.dma_start(list_of_tz[:], offs6)
        nc.sync.dma_start(out=sx_w[:].bitcast(I32), in_=fp8_words(sx_words))
        nc.sync.dma_start(out=ws_w[:].bitcast(I32), in_=fp8_words(ws_words))
        nc.sync.dma_start(out=wb_w[:].bitcast(I32), in_=wb_words[0].bitcast(I32))

        nc.vector.tensor_copy(out=w_s[:].rearrange("p (t m) -> p t m", t=PACK),
                              in_=w_s_given[:].rearrange("p (m t) -> p t m", t=PACK))
        for u in range(PACK // 2):
            nc.scalar.copy(out=w_w[:, u * 2 * P:(u + 1) * 2 * P].rearrange("p (t m) -> p m t", t=2),
                           in_=w_w_given[:].rearrange("p (m t) -> p m t", t=PACK)[:, :, 2 * u:2 * u + 2])

        names = ("a", "b", "g")
        tok_w = [sb.tile([P, J], U16, name="tok_w_" + s, align_bytes=MX_ALIGN) for s in names]
        tok_s = [sb.tile([P, J], U8, name="tok_s_" + s, align_bytes=MX_ALIGN) for s in names]
        for s, entries in enumerate((list_a, list_b, list_g)):
            nc.vector.tensor_copy(out=tok_w[s][:], in_=xt_w[:].indirect(entries[:]))
            nc.vector.tensor_copy(out=tok_s[s][:], in_=xt_s[:].indirect(entries[:]))

        def first_stage(result, s, t):
            cols = slice(t * P, (t + 1) * P)
            nc.tensor.matmul_mx(out=result, lhsT=w_w[:, cols].bitcast(E4M3), lhsT_scale=w_s[:, cols],
                                rhs=tok_w[s][:].bitcast(E2M1), rhs_scale=tok_s[s][:], start=True, stop=True)

        a_slices = []
        for t in range(PACK):
            bank = ps.tile([P, J], F32, name="a_bank%d" % t, tag="slice_bank%d" % t)
            first_stage(bank[:], 0, t)
            a_slice = sb.tile([P, J], F32, name="a_slice%d" % t)
            nc.scalar.copy(out=a_slice[:], in_=bank[:])
            a_slices.append(a_slice)
        b_pairs = []
        for u in range(PACK // 2):
            bank = ps.tile([P, 2, J], F32, name="b_bank%d" % u)
            for v in range(2):
                first_stage(bank[:, v, :], 1, 2 * u + v)
            b_pair = sb.tile([P, 2, J], F32, name="b_pair%d" % u, tag="b_pair%d" % u)
            nc.scalar.copy(out=b_pair[:], in_=bank[:])
            b_pairs.append(b_pair)

        a_picked = sb.tile([P, PACK, O], F32, name="a_picked")
        c_picked = sb.tile([P, PACK, O], F32, name="c_picked")
        for t in range(PACK):
            pick(nc, t < A_PICKS_ON_SCALAR, a_picked[:, t, :], a_slices[t][:], list_of_a[:])
        c_slices = []
        for t in range(PACK):
            bank = ps.tile([P, J], F32, name="g_bank%d" % t, tag="slice_bank%d" % t)
            first_stage(bank[:], 2, t)
            c_slice = sb.tile([P, J], F32, name="c_slice%d" % t)
            nc.vector.tensor_tensor(out=c_slice[:], in0=bank[:], in1=b_pairs[t // 2][:, t % 2, :], op=MAX)
            c_slices.append(c_slice)
        for t in range(PACK):
            pick(nc, t < C_PICKS_ON_SCALAR, c_picked[:, t, :], c_slices[t][:], list_of_c[:])

        hid = sb.tile([P, O * PACK], BF16, name="hid", align_bytes=MX_ALIGN)
        hid_w = sb.tile([P, O], U32, name="hid_w", align_bytes=MX_ALIGN)
        hid_s = sb.tile([P, O], U8, name="hid_s", align_bytes=MX_ALIGN)
        half = O // 2
        for u in range(2):
            places = slice(u * half, (u + 1) * half)
            nc.vector.tensor_tensor(
                out=hid[:, u * half * PACK:(u + 1) * half * PACK].rearrange("p (c i t) -> p c t i", i=4, t=PACK),
                in0=a_picked[:, :, places].rearrange("p t (c i) -> p c t i", i=4),
                in1=c_picked[:, :, places].rearrange("p t (c i) -> p c t i", i=4), op=MAX)
        for u in range(2):
            places = slice(u * half, (u + 1) * half)
            nc.vector.quantize_mx(out=hid_w[:, places].bitcast(E5M2), scales=hid_s[:, places],
                                  in_=hid[:, u * half * PACK:(u + 1) * half * PACK])

        tz_picked = sb.tile([P, N // P, O], F32, name="tz_picked", tag="b_pair1")
        for h in range(N // P):
            pick(nc, True, tz_picked[:, h, :], tz_rows[h][:], list_of_tz[:])

        sums = [ps.tile([P, O], F32, name="sum%d" % h) for h in range(N // P)]
        for h in range(N // P):
            cols = slice(h * P, (h + 1) * P)
            nc.tensor.matmul_mx(out=sums[h][:], lhsT=ws_w[:, cols].bitcast(E4M3), lhsT_scale=ws_s[:, cols],
                                rhs=sx_w[:].bitcast(E4M3), rhs_scale=sx_s, start=True, stop=False)
        for h in range(N // P):
            cols = slice(h * P, (h + 1) * P)
            nc.tensor.matmul_mx(out=sums[h][:], lhsT=wb_w[:, cols].bitcast(E2M1), lhsT_scale=wb_s[:, cols],
                                rhs=hid_w[:].bitcast(E5M2), rhs_scale=hid_s[:], start=False, stop=True)
            result = sb.tile([P, O], F32, name="result%d" % h)
            nc.vector.tensor_tensor(out=result[:], in0=sums[h][:], in1=tz_picked[:, h, :], op=ADD)
            (nc.sync, nc.scalar)[h].dma_start(out=out[cols, :], in_=result[:])
